import numpy as np, ml_dtypes
CORES = [2,6,18,22,34,38,50,54,66,70,82,86,98,102,114,118]
N = 16
def setup_inputs(rng):
    return {"x": rng.standard_normal((N, 128, 8), dtype=np.float32).astype(ml_dtypes.bfloat16)}
def reference(x):
    g = np.ascontiguousarray(x.transpose(1, 2, 0)).reshape(128, 8 * N)
    return {"y": np.broadcast_to(g, (N,) + g.shape)}

from concourse.bass import DstId, RemoteDMATransfer

N = 16
SCRATCH = {
    "xd": ("dram", [8, 128, 1], "bfloat16"),
    "land": ("dram", [16, 128, 1], "bfloat16"),
    "w": ("sbuf", [128, 16], "bfloat16"),
    "ybuf": ("dram", [8, 128, 16], "bfloat16"),
}
SEMAPHORES = ["loaded", "sent1", "got1", "turned", "sent2", "got2", "own", "stored"]


def rank_program(g, core, T, topo):
    chips = sorted(set(topo.chip(c) for c in T.cores))
    if topo.chip(core) not in chips:
        return
    sem = T.sem
    me = T.rank_of(core)
    t = core % 8

    def dst_id(c):
        rid, pid, _se = topo.addr(c)
        return DstId(rid=rid, pnc=pid)

    if me is not None:
        g.sync.dma_start(T.xd[:], T.x[:]).then_inc(sem.loaded, 16)
        g.wait_ge(sem.loaded, 16)
        trs = []
        for k in range(8):
            dsts = [ch * 8 + k for ch in chips if ch * 8 + k != core]
            trs.append(RemoteDMATransfer(dst_ids=[dst_id(c) for c in dsts], dma_engine_mask=1 << k,
                                         remote_sem=sem.got1, srcs=[T.xd[k]], dsts=[T.land[me] for c in dsts]))
        g.remote_dma_fused(trs, local_sem=sem.sent1)
        g.sync.wait_ge(sem.loaded, 16)
        g.sync.dma_start(T.w[:, me:me + 1], T.xd[t]).then_inc(sem.turned, 16)

    senders = [r for r in range(N) if r != me]
    g.sync.wait_ge(sem.got1, len(senders))
    g.scalar.wait_ge(sem.got1, len(senders))
    for i, r in enumerate(senders):
        q = g.scalar if i % 2 == 0 else g.sync
        q.dma_start(T.w[:, r:r + 1], T.land[r]).then_inc(sem.turned, 16)
    g.wait_ge(sem.turned, 16 * N)

    ranks_here = [c for c in T.cores if topo.chip(c) == topo.chip(core) and c != core]
    g.remote_dma_fused([RemoteDMATransfer(dst_ids=[dst_id(c) for c in ranks_here], dma_engine_mask=0xFFFF,
                                          remote_sem=sem.got2, srcs=[T.w[:]], dsts=[T.ybuf[t] for c in ranks_here])],
                       local_sem=sem.sent2)
    if me is not None:
        g.sync.wait_ge(sem.turned, 16 * N)
        g.sync.dma_start(T.ybuf[t], T.w[:]).then_inc(sem.own, 16)
        g.sync.wait_ge(sem.own, 16)
        g.sync.wait_ge(sem.got2, 16 * 7)
        g.sync.dma_start(T.y[:], T.ybuf[:]).then_inc(sem.stored, 16)
        g.wait_ge(sem.sent1, 8)
        g.wait_ge(sem.stored, 16)
    g.wait_ge(sem.sent2, 16)
